import numpy as np
import ml_dtypes


def mxq(x, axis, fmt="e4m3"):
    dtype, down = {"e4m3": (ml_dtypes.float8_e4m3fn, 7), "e5m2": (ml_dtypes.float8_e5m2, 14)}[fmt]
    v = np.moveaxis(np.asarray(x, np.float32).astype(ml_dtypes.bfloat16).astype(np.float64), axis, -1)
    blocks = v.reshape(v.shape[:-1] + (-1, 32))
    amax = np.abs(blocks).max(-1, keepdims=True)
    byte = np.maximum(np.where(amax > 0, np.frexp(amax)[1] - 1 + 127, 0) - down, 1)
    scale = np.exp2(byte - 127.0)
    codes = (blocks / scale).astype(np.float32).astype(dtype).astype(np.float64)
    return np.moveaxis((codes * scale).reshape(v.shape), -1, axis)


WIDE = False


def mx_kscale(k):
    if not WIDE:
        return np.ones(k)
    levels = np.array([30, -30])
    if k % 512:
        return np.exp2(np.random.permutation(np.resize(levels, k // 32))).repeat(32)
    a = np.empty((k // 512, 16))
    for p in range(k // 512):
        a[p, :8] = np.random.permutation(np.resize(levels, 8))
        for g in range(8):
            far = levels[np.abs(levels - a[p, g]) >= 10]
            a[p, g + 8] = far[np.random.randint(len(far))]
    return np.exp2(a.ravel()).repeat(32)


BF16 = ml_dtypes.bfloat16


def bf(x):
    return np.asarray(x, np.float32).astype(BF16)


def f64(x):
    return np.asarray(x).astype(np.float64)


M, K, T, N = 2048, 2048, 1024, 512


def setup_inputs():
    s, t = mx_kscale(K), mx_kscale(T)
    row_mean = bf(0.3 * np.random.standard_normal(M))
    oe = np.exp(np.random.standard_normal((M, K)) + f64(row_mean)[:, None])
    tail = np.exp(0.7 * np.random.standard_normal((M, T)))
    return {"oe": bf(oe),
            "row_mean": row_mean,
            "bin_weight": bf((1 + 0.1 * np.random.standard_normal(K)) * s),
            "trans": bf(np.random.standard_normal((M, T)) * tail * t),
            "cis_load": bf(np.random.standard_normal((K, N)) / np.sqrt(K) / s[:, None]),
            "trans_load": bf(np.random.standard_normal((T, N)) / np.sqrt(T) / t[:, None]),
            "inv_sd": bf(1 + 0.1 * np.random.standard_normal(M)),
            "inv_root": bf(1 + 0.1 * np.random.standard_normal(N))}


def reference(oe, row_mean, bin_weight, trans, cis_load, trans_load, inv_sd, inv_root):
    z = (np.log(f64(oe)) - f64(row_mean)[:, None]) * f64(bin_weight)
    cis = mxq(z, 1, "e4m3") @ mxq(f64(cis_load), 0, "e4m3")
    far = mxq(f64(trans), 1, "e5m2") @ mxq(f64(trans_load), 0, "e4m3")
    return (cis + far) * f64(inv_sd)[:, None] * f64(inv_root)

@@ -1,0 +1,420 @@
+from contextlib import ExitStack
+
+import concourse.mybir as mybir
+from concourse.masks import make_identity
+
+M, K, T, N = 2048, 2048, 1024, 512
+FLOPS = 2 * M * (K + T) * N
+
+F32 = mybir.dt.float32
+BF16 = mybir.dt.bfloat16
+U32 = mybir.dt.uint32
+U8 = mybir.dt.uint8
+E4M3 = mybir.dt.float8_e4m3fn_x4
+E5M2 = mybir.dt.float8_e5m2_x4
+LN = mybir.ActivationFunctionType.Ln
+SUB = mybir.AluOpType.subtract
+ADD = mybir.AluOpType.add
+MULT = mybir.AluOpType.mult
+
+P = 128
+PACK = 4
+K_PASS = P * PACK
+TILES = M // P
+CIS_PASSES = K // K_PASS
+FAR_PASSES = T // K_PASS
+PASSES = CIS_PASSES + FAR_PASSES
+CATCH = 10
+TAPER = 11
+GW4 = 1
+TM = 4
+LEAD = 1
+GP = 256
+G_FROM = 3
+G_TO = 14
+V_EMPTY = 3
+SPLIT = 0
+TURN = 4
+GW = 1
+VG = 0
+
+
+def tile_hic_compartment_scores_s2_kernel(
+    tc, oe, row_mean, bin_weight, trans, cis_load, trans_load, inv_sd, inv_root, out
+):
+    nc = tc.nc
+    oe_rows = oe.rearrange("(p j) k -> p j k", j=TILES)
+    trans_rows = trans.rearrange("(p j) k -> p j k", j=TILES)
+    out_rows = out.rearrange("(p j) c -> p j c", j=TILES)
+
+    with ExitStack() as ctx:
+        keep = ctx.enter_context(tc.tile_pool(name="keep", bufs=1))
+        work = ctx.enter_context(tc.tile_pool(name="work", bufs=2))
+        psum = ctx.enter_context(tc.psum_pool(name="psum", bufs=2))
+        ctx.enter_context(tc.manual_schedule())
+
+        ident = keep.tile([P, P], F32, name="ident")
+        mean_col = keep.tile([P, TILES], BF16, name="mean_col")
+        sd_col = keep.tile([P, TILES], BF16, name="sd_col")
+        weight_col = keep.tile([P, K // P], BF16, name="weight_col")
+        root_col = keep.tile([P, N // P], BF16, name="root_col")
+        weight_row = keep.tile([P, 2, max(GP, 16)], BF16, name="weight_row", align_bytes=64)
+        weight_bank = {}
+        gate_slot = {}
+        root_row = keep.tile([P, N], BF16, name="root_row", align_bytes=64)
+
+        oe_t, tr_t, ln_t, z_t, zbank, tbank, zg, tg, zq, tq, acc, res = ({} for i in range(12))
+        w_raw, w_int, w_q = {}, {}, {}
+
+        def load_oe(j, parts=1):
+            tiles = []
+            width = K // parts
+            for h in range(parts):
+                if parts == 1:
+                    t = work.tile([P, width], BF16, name="oe", bufs=6)
+                else:
+                    t = work.tile([P, width], BF16, name="oe_part", bufs=4)
+                nc.sync.dma_start(out=t[:], in_=oe_rows[:, j, h * width : (h + 1) * width])
+                tiles.append(t)
+            oe_t[j] = tiles
+
+        def load_trans(j):
+            tr_t[j] = work.tile([P, T], BF16, name="tr", bufs=6)
+            nc.sync.dma_start(out=tr_t[j][:], in_=trans_rows[:, j, :])
+
+        def load_w(g):
+            src = cis_load if g < CIS_PASSES else trans_load
+            g0 = g if g < CIS_PASSES else g - CIS_PASSES
+            w_raw[g] = work.tile([P, PACK * N], BF16, name="w_raw", bufs=PASSES)
+            nc.sync.dma_start(
+                out=w_raw[g][:],
+                in_=src[g0 * K_PASS : (g0 + 1) * K_PASS, :].rearrange("(p t) c -> p (t c)", t=PACK),
+            )
+
+        def g_copy(out, in_):
+            nc.gpsimd.tensor_scalar(out=out, in0=in_, scalar1=1.0, scalar2=0.0, op0=MULT, op1=ADD)
+
+        def interleave_w(g, copy):
+            w_int[g] = work.tile([P, N * PACK], BF16, name="w_int", tag="wi%d" % min(g, 7 - g), bufs=1, align_bytes=64)
+            copy(
+                out=w_int[g][:].rearrange("p (c i t) -> p c t i", i=4, t=PACK),
+                in_=w_raw[g][:].rearrange("p (t c i) -> p c t i", i=4, t=PACK),
+            )
+
+        def quantize_w(g):
+            codes = keep.tile([P, N], U32, name="w_codes", bufs=PASSES, align_bytes=64)
+            scales = keep.tile([P, N], U8, name="w_scales", bufs=PASSES, align_bytes=64)
+            nc.vector.quantize_mx(out=codes[:].bitcast(E4M3), scales=scales[:], in_=w_int[g][:])
+            w_q[g] = (codes, scales)
+
+        def spread(col, a, dst):
+            words = col[:].bitcast(F32)
+            nc.tensor.transpose(dst, words[:, a : a + 1].to_broadcast([P, P]), ident[:])
+
+        def weight_table(u):
+            weight_bank[u] = psum.tile([P, 512], F32, name="wbank", bufs=2)
+            for a in range(4):
+                spread(weight_col, 2 * a + u, weight_bank[u][:, a:512:4])
+
+        def weight_share(u):
+            nc.vector.tensor_copy(
+                out=weight_row[:, u, :].bitcast(F32), in_=weight_bank[u][:, 512 - GP // 2 : 512]
+            )
+
+        def root_table():
+            bank = psum.tile([P, 4, P], F32, name="turn", bufs=TURN)
+            for a in range(2):
+                spread(root_col, a, bank[:, a, :])
+            nc.vector.tensor_copy(
+                out=root_row[:].bitcast(F32).rearrange("p (n a) -> p n a", a=2),
+                in_=bank[:, 0:2, :].rearrange("p a n -> p n a"),
+            )
+
+        def log_of(j, h=0, parts=1):
+            if h == 0:
+                ln_t[j] = work.tile([P, K], F32, name="ln", bufs=4)
+            pairs = K // PACK // parts
+            src = oe_t[j][h] if len(oe_t[j]) > 1 else oe_t[j][0][:, h * (K // parts) : (h + 1) * (K // parts)]
+            nc.scalar.activation(
+                out=ln_t[j][:].rearrange("p (u m e) -> p u m e", u=2, e=2)[:, :, h * pairs : (h + 1) * pairs, :],
+                in_=src[:].rearrange("p (m u e) -> p u m e", u=2, e=2),
+                func=LN,
+            )
+
+        def centre(j, c0, c1):
+            if c0 == 0:
+                z_t[j] = work.tile([P, K], BF16, name="z", bufs=3)
+            for u in range(2):
+                cols = slice(u * 1024 + c0, u * 1024 + c1)
+                nc.vector.scalar_tensor_tensor(
+                    out=z_t[j][:, cols],
+                    in0=ln_t[j][:, cols],
+                    scalar=mean_col[:, j : j + 1],
+                    in1=weight_bank[u][:].bitcast(BF16)[:, c0:c1],
+                    op0=SUB,
+                    op1=MULT,
+                )
+
+        def centre_share(j):
+            diff = work.tile([P, 2, GP], F32, name="diff", tag="tg%d" % (j % 2), bufs=1, align_bytes=64)
+            nc.gpsimd.tensor_scalar(
+                out=diff[:],
+                in0=ln_t[j][:].rearrange("p (u x) -> p u x", u=2)[:, :, 1024 - GP : 1024],
+                scalar1=mean_col[:, j : j + 1],
+                scalar2=1.0,
+                op0=SUB,
+                op1=MULT,
+            )
+            nc.gpsimd.tensor_tensor(
+                out=z_t[j][:].rearrange("p (u x) -> p u x", u=2)[:, :, 1024 - GP : 1024],
+                in0=diff[:],
+                in1=weight_row[:],
+                op=MULT,
+            )
+
+        def turn_z(j, h):
+            words = z_t[j][:].bitcast(F32)
+            zbank[j, h] = psum.tile([P, 4, P], F32, name="turn", bufs=TURN)
+            for g in range(2):
+                for u in range(2):
+                    c0 = u * 512 + (2 * h + g) * P
+                    nc.tensor.transpose(zbank[j, h][:, 2 * g + u, :], words[:, c0 : c0 + P], ident[:])
+
+        def turn_trans(j):
+            words = tr_t[j][:].bitcast(F32)
+            tbank[j] = psum.tile([P, 4, P], F32, name="turn", bufs=TURN)
+            for g in range(2):
+                for u in range(2):
+                    nc.tensor.transpose(
+                        tbank[j][:, 2 * g + u, :], words[:, 256 * g + u : 256 * (g + 1) : 2], ident[:]
+                    )
+
+        def empty(bank, dst, copy):
+            copy(
+                out=dst.bitcast(F32).rearrange("p (g r u) -> p g r u", g=2, u=2),
+                in_=bank[:].rearrange("p (g u) r -> p g r u", u=2),
+            )
+
+        def empty_z(j, h, copy=nc.scalar.copy):
+            if h == 0:
+                zg[j] = work.tile([P, K], BF16, name="zg", bufs=4, align_bytes=64)
+            empty(zbank[j, h], zg[j][:, h * 1024 : (h + 1) * 1024], copy)
+
+        def empty_trans(j, copy=nc.scalar.copy):
+            tg[j] = work.tile([P, T], BF16, name="tg", tag="tg%d" % (j % 2), bufs=1, align_bytes=64)
+            empty(tbank[j], tg[j][:], copy)
+
+        def quantize_z(j, h=0, parts=1):
+            if h == 0:
+                codes = work.tile([P, K // PACK], U32, name="z_codes", bufs=4, align_bytes=64)
+                scales = work.tile([P, K // PACK], U8, name="z_scales", bufs=4, align_bytes=64)
+                zq[j] = (codes, scales)
+            codes, scales = zq[j]
+            w = K // PACK // parts
+            nc.vector.quantize_mx(
+                out=codes[:, h * w : (h + 1) * w].bitcast(E4M3),
+                scales=scales[:, h * w : (h + 1) * w],
+                in_=zg[j][:, h * w * PACK : (h + 1) * w * PACK],
+            )
+
+        def quantize_trans(j):
+            codes = work.tile([P, T // PACK], U32, name="t_codes", bufs=4, align_bytes=64)
+            scales = work.tile([P, T // PACK], U8, name="t_scales", bufs=4, align_bytes=64)
+            nc.vector.quantize_mx(out=codes[:].bitcast(E5M2), scales=scales[:], in_=tg[j][:])
+            tq[j] = (codes, scales)
+
+        def multiply(j, order, lo=0, hi=PASSES):
+            if lo == 0 and j == TILES - 1:
+                acc[j] = psum.tile([P, N], F32, name="turn", bufs=TURN)
+            elif lo == 0:
+                acc[j] = psum.tile([P, N], F32, name="acc", bufs=6 - TURN)
+            for g in order[lo:hi]:
+                if g < CIS_PASSES:
+                    (codes, scales), fmt, c0 = zq[j], E4M3, g * P
+                else:
+                    (codes, scales), fmt, c0 = tq[j], E5M2, (g - CIS_PASSES) * P
+                nc.tensor.matmul_mx(
+                    out=acc[j][:],
+                    lhsT=codes[:, c0 : c0 + P].bitcast(fmt),
+                    lhsT_scale=scales[:, c0 : c0 + P],
+                    rhs=w_q[g][0][:].bitcast(E4M3),
+                    rhs_scale=w_q[g][1][:],
+                    start=(g == order[0]),
+                    stop=(g == order[-1]),
+                )
+
+        def finish(j):
+            res[j] = work.tile([P, N], F32, name="res", bufs=4)
+            nc.vector.scalar_tensor_tensor(
+                out=res[j][:],
+                in0=acc[j][:],
+                scalar=sd_col[:, j : j + 1],
+                in1=root_row[:],
+                op0=MULT,
+                op1=MULT,
+            )
+            nc.sync.dma_start(out=out_rows[:, j, :], in_=res[j][:])
+
+        far_first = [4, 5, 0, 1, 2, 3]
+        v_copy, s_copy = nc.vector.tensor_copy, nc.scalar.copy
+
+        make_identity(nc, ident[:])
+        nc.sync.dma_start(out=weight_col[:], in_=bin_weight.rearrange("(p a) -> p a", p=P))
+        load_oe(0, parts=4)
+        nc.sync.dma_start(out=mean_col[:], in_=row_mean.rearrange("(p j) -> p j", p=P))
+        load_oe(1)
+        load_w(0)
+        load_w(1)
+        load_w(2)
+        load_trans(0)
+        load_w(3)
+        load_oe(2)
+        load_w(4)
+        load_w(5)
+        load_trans(1)
+        nc.sync.dma_start(out=root_col[:], in_=inv_root.rearrange("(p a) -> p a", p=P))
+        nc.sync.dma_start(out=sd_col[:], in_=inv_sd.rearrange("(p j) -> p j", p=P))
+        load_oe(3)
+        load_trans(2)
+        load_oe(4)
+        load_trans(3)
+        load_oe(5)
+        load_trans(4)
+
+        weight_table(0)
+        weight_table(1)
+        for h in range(4):
+            log_of(0, h, 4)
+        centre(0, 0, 256)
+        centre(0, 256, 512)
+        centre(0, 512, 1024)
+        log_of(1, 0, 2)
+        log_of(1, 1, 2)
+        if GP:
+            weight_share(0)
+            weight_share(1)
+        interleave_w(0, g_copy if GW else v_copy)
+        centre(1, 0, 512)
+        centre(1, 512, 1024)
+        cis_first = [0, 1, 2, 3, 4, 5]
+        turn_z(0, 0)
+        turn_z(0, 1)
+        empty_z(0, 0)
+        empty_z(0, 1)
+        turn_z(1, 0)
+        turn_z(1, 1)
+        turn_trans(0)
+        interleave_w(1, s_copy)
+        interleave_w(2, v_copy)
+        quantize_w(0)
+        quantize_z(0)
+        multiply(0, cis_first, 0, 1)
+        empty_z(1, 0)
+        empty_z(1, 1)
+        interleave_w(3, v_copy)
+        quantize_w(1)
+        quantize_w(2)
+        multiply(0, cis_first, 1, 3)
+        quantize_z(1)
+        multiply(1, cis_first, 0, 3)
+        log_of(2)
+        empty_trans(0)
+        if not GW4:
+            interleave_w(4, v_copy)
+        quantize_w(3)
+        multiply(0, cis_first, 3, 4)
+        multiply(1, cis_first, 3, 4)
+        if GW4:
+            interleave_w(4, g_copy)
+        turn_trans(1)
+        interleave_w(5, s_copy)
+        centre(2, 0, 1024)
+        root_table()
+        empty_trans(1, v_copy)
+        quantize_trans(0)
+        quantize_w(4)
+        quantize_w(5)
+        turn_z(2, 0)
+        turn_z(2, 1)
+        turn_trans(2)
+        multiply(0, cis_first, 4, 6)
+        log_of(3)
+        empty_z(2, 0)
+        empty_z(2, 1)
+        empty_trans(2)
+
+        turn_trans(3)
+        last = TILES - 1
+
+        def on_vector(s):
+            return V_EMPTY and s > 2 and (s % V_EMPTY == 0) == VG
+
+        def centre_step(s):
+            if GP and G_FROM <= s <= G_TO:
+                centre(s, 0, 1024 - GP)
+                centre_share(s)
+            else:
+                centre(s, 0, 1024)
+
+        def load_step(s):
+            if s + 2 < TILES:
+                load_trans(s + 2)
+            if s + 3 < TILES:
+                load_oe(s + 3)
+
+        for s in range(3, last):
+            load_step(s)
+            if s > 4:
+                quantize_z(s - 3)
+            quantize_trans(s - 2)
+            if s == 3:
+                multiply(1, cis_first, 4, 6)
+            elif s > 4:
+                multiply(s - 3, far_first, 2)
+            centre_step(s)
+            log_of(s + 1, 0, 1 if s + 1 < last else 2)
+            if on_vector(s - 1):
+                empty_trans(s - 1, v_copy)
+            finish(s - 3)
+            if s > 3:
+                turn_z(s - 1, 0)
+                turn_z(s - 1, 1)
+                turn_trans(s)
+                if s + 1 < last:
+                    multiply(s - 2, far_first, 0, 2)
+                if s + 1 == last:
+                    log_of(last, 1, 2)
+                empty_z(s - 1, 0)
+                empty_z(s - 1, 1)
+            if not on_vector(s):
+                empty_trans(s)
+        quantize_z(last - 3)
+        multiply(last - 3, far_first)
+        if on_vector(last - 1):
+            empty_trans(last - 1)
+        turn_z(last - 1, 0)
+        turn_z(last - 1, 1)
+        centre(last, 0, 512)
+        quantize_z(last - 2)
+        quantize_trans(last - 2)
+        centre(last, 512, 1024)
+        empty_z(last - 1, 0)
+        empty_z(last - 1, 1)
+        turn_trans(last)
+        turn_z(last, 0)
+        finish(last - 3)
+        multiply(last - 2, far_first, 0, TM)
+        empty_trans(last)
+        empty_z(last, 0)
+        turn_z(last, 1)
+        empty_z(last, 1)
+        multiply(last - 2, far_first, TM)
+        quantize_trans(last - 1)
+        quantize_z(last - 1)
+        multiply(last - 1, far_first)
+        quantize_trans(last)
+        quantize_z(last)
+        finish(last - 2)
+        multiply(last, far_first)
+        finish(last - 1)
+        finish(last)

@@ -26,17 +26,18 @@ FAR_PASSES = T // K_PASS
 PASSES = CIS_PASSES + FAR_PASSES
 CATCH = 10
 TAPER = 11
-GW4 = 1
+GC = 384
+GC4 = 384
 TM = 4
 LEAD = 1
-GP = 256
+GP = 192
 G_FROM = 3
 G_TO = 14
-V_EMPTY = 3
+V_EMPTY = 2
 SPLIT = 0
 TURN = 4
 GW = 1
-VG = 0
+VG = 1
 
 
 def tile_hic_compartment_scores_s2_kernel(
@@ -55,6 +56,7 @@ def tile_hic_compartment_scores_s2_kernel(
 
         ident = keep.tile([P, P], F32, name="ident")
         mean_col = keep.tile([P, TILES], BF16, name="mean_col")
+        minus_mean = keep.tile([P, TILES], F32, name="minus_mean")
         sd_col = keep.tile([P, TILES], BF16, name="sd_col")
         weight_col = keep.tile([P, K // P], BF16, name="weight_col")
         root_col = keep.tile([P, N // P], BF16, name="root_col")
@@ -94,11 +96,12 @@ def tile_hic_compartment_scores_s2_kernel(
         def g_copy(out, in_):
             nc.gpsimd.tensor_scalar(out=out, in0=in_, scalar1=1.0, scalar2=0.0, op0=MULT, op1=ADD)
 
-        def interleave_w(g, copy):
-            w_int[g] = work.tile([P, N * PACK], BF16, name="w_int", tag="wi%d" % min(g, 7 - g), bufs=1, align_bytes=64)
+        def interleave_w(g, copy, c0=0, c1=N):
+            if c0 == 0:
+                w_int[g] = work.tile([P, N * PACK], BF16, name="w_int", tag="wi%d" % min(g, 7 - g), bufs=1, align_bytes=64)
             copy(
-                out=w_int[g][:].rearrange("p (c i t) -> p c t i", i=4, t=PACK),
-                in_=w_raw[g][:].rearrange("p (t c i) -> p c t i", i=4, t=PACK),
+                out=w_int[g][:].rearrange("p (c i t) -> p c t i", i=4, t=PACK)[:, c0 // 4 : c1 // 4],
+                in_=w_raw[g][:].rearrange("p (t c i) -> p c t i", i=4, t=PACK)[:, c0 // 4 : c1 // 4],
             )
 
         def quantize_w(g):
@@ -160,9 +163,9 @@ def tile_hic_compartment_scores_s2_kernel(
             nc.gpsimd.tensor_scalar(
                 out=diff[:],
                 in0=ln_t[j][:].rearrange("p (u x) -> p u x", u=2)[:, :, 1024 - GP : 1024],
-                scalar1=mean_col[:, j : j + 1],
+                scalar1=minus_mean[:, j : j + 1],
                 scalar2=1.0,
-                op0=SUB,
+                op0=ADD,
                 op1=MULT,
             )
             nc.gpsimd.tensor_tensor(
@@ -260,8 +263,8 @@ def tile_hic_compartment_scores_s2_kernel(
 
         make_identity(nc, ident[:])
         nc.sync.dma_start(out=weight_col[:], in_=bin_weight.rearrange("(p a) -> p a", p=P))
-        load_oe(0, parts=4)
         nc.sync.dma_start(out=mean_col[:], in_=row_mean.rearrange("(p j) -> p j", p=P))
+        load_oe(0, parts=4)
         load_oe(1)
         load_w(0)
         load_w(1)
@@ -285,6 +288,7 @@ def tile_hic_compartment_scores_s2_kernel(
         weight_table(1)
         for h in range(4):
             log_of(0, h, 4)
+        nc.vector.tensor_scalar(out=minus_mean[:], in0=mean_col[:], scalar1=-1.0, scalar2=None, op0=MULT)
         centre(0, 0, 256)
         centre(0, 256, 512)
         centre(0, 512, 1024)
@@ -293,7 +297,7 @@ def tile_hic_compartment_scores_s2_kernel(
         if GP:
             weight_share(0)
             weight_share(1)
-        interleave_w(0, g_copy if GW else v_copy)
+        interleave_w(0, g_copy, 0, GC)
         centre(1, 0, 512)
         centre(1, 512, 1024)
         cis_first = [0, 1, 2, 3, 4, 5]
@@ -306,6 +310,8 @@ def tile_hic_compartment_scores_s2_kernel(
         turn_trans(0)
         interleave_w(1, s_copy)
         interleave_w(2, v_copy)
+        if GC < N:
+            interleave_w(0, v_copy, GC, N)
         quantize_w(0)
         quantize_z(0)
         multiply(0, cis_first, 0, 1)
@@ -319,18 +325,17 @@ def tile_hic_compartment_scores_s2_kernel(
         multiply(1, cis_first, 0, 3)
         log_of(2)
         empty_trans(0)
-        if not GW4:
-            interleave_w(4, v_copy)
         quantize_w(3)
         multiply(0, cis_first, 3, 4)
         multiply(1, cis_first, 3, 4)
-        if GW4:
-            interleave_w(4, g_copy)
+        interleave_w(4, g_copy, 0, GC4)
         turn_trans(1)
         interleave_w(5, s_copy)
         centre(2, 0, 1024)
         root_table()
         empty_trans(1, v_copy)
+        if GC4 < N:
+            interleave_w(4, v_copy, GC4, N)
         quantize_trans(0)
         quantize_w(4)
         quantize_w(5)

@@ -29,9 +29,16 @@ TAPER = 11
 GC = 384
 GC4 = 384
 TM = 4
+AT = 2
+ET = 10
+LS = 13
+SW = 0
+LD = 2
+FL = 4
+SR = 2
 LEAD = 1
-GP = 192
-G_FROM = 3
+GP = 208
+G_FROM = 5
 G_TO = 14
 V_EMPTY = 2
 SPLIT = 0
@@ -65,7 +72,7 @@ def tile_hic_compartment_scores_s2_kernel(
         gate_slot = {}
         root_row = keep.tile([P, N], BF16, name="root_row", align_bytes=64)
 
-        oe_t, tr_t, ln_t, z_t, zbank, tbank, zg, tg, zq, tq, acc, res = ({} for i in range(12))
+        oe_t, tr_t, ln_t, z_t, zbank, tbank, zg, tg, zq, tq, acc = ({} for i in range(11))
         w_raw, w_int, w_q = {}, {}, {}
 
         def load_oe(j, parts=1):
@@ -81,7 +88,7 @@ def tile_hic_compartment_scores_s2_kernel(
             oe_t[j] = tiles
 
         def load_trans(j):
-            tr_t[j] = work.tile([P, T], BF16, name="tr", bufs=6)
+            tr_t[j] = work.tile([P, T], BF16, name="tr", bufs=7)
             nc.sync.dma_start(out=tr_t[j][:], in_=trans_rows[:, j, :])
 
         def load_w(g):
@@ -98,7 +105,7 @@ def tile_hic_compartment_scores_s2_kernel(
 
         def interleave_w(g, copy, c0=0, c1=N):
             if c0 == 0:
-                w_int[g] = work.tile([P, N * PACK], BF16, name="w_int", tag="wi%d" % min(g, 7 - g), bufs=1, align_bytes=64)
+                w_int[g] = work.tile([P, N * PACK], BF16, name="w_int", tag="wi%d" % (g in (1, 2)), bufs=1, align_bytes=64)
             copy(
                 out=w_int[g][:].rearrange("p (c i t) -> p c t i", i=4, t=PACK)[:, c0 // 4 : c1 // 4],
                 in_=w_raw[g][:].rearrange("p (t c i) -> p c t i", i=4, t=PACK)[:, c0 // 4 : c1 // 4],
@@ -204,7 +211,7 @@ def tile_hic_compartment_scores_s2_kernel(
             empty(zbank[j, h], zg[j][:, h * 1024 : (h + 1) * 1024], copy)
 
         def empty_trans(j, copy=nc.scalar.copy):
-            tg[j] = work.tile([P, T], BF16, name="tg", tag="tg%d" % (j % 2), bufs=1, align_bytes=64)
+            tg[j] = work.tile([P, T], BF16, name="tg", tag="tg%d" % (j % 2 if j < TILES - 2 else j), bufs=1, align_bytes=64)
             empty(tbank[j], tg[j][:], copy)
 
         def quantize_z(j, h=0, parts=1):
@@ -227,7 +234,7 @@ def tile_hic_compartment_scores_s2_kernel(
             tq[j] = (codes, scales)
 
         def multiply(j, order, lo=0, hi=PASSES):
-            if lo == 0 and j == TILES - 1:
+            if lo == 0 and j >= TILES - AT:
                 acc[j] = psum.tile([P, N], F32, name="turn", bufs=TURN)
             elif lo == 0:
                 acc[j] = psum.tile([P, N], F32, name="acc", bufs=6 - TURN)
@@ -246,17 +253,17 @@ def tile_hic_compartment_scores_s2_kernel(
                     stop=(g == order[-1]),
                 )
 
-        def finish(j):
-            res[j] = work.tile([P, N], F32, name="res", bufs=4)
+        def finish(j, c0=0, c1=N):
+            res = work.tile([P, c1 - c0], F32, name="res", bufs=6)
             nc.vector.scalar_tensor_tensor(
-                out=res[j][:],
-                in0=acc[j][:],
+                out=res[:],
+                in0=acc[j][:, c0:c1],
                 scalar=sd_col[:, j : j + 1],
-                in1=root_row[:],
+                in1=root_row[:, c0:c1],
                 op0=MULT,
                 op1=MULT,
             )
-            nc.sync.dma_start(out=out_rows[:, j, :], in_=res[j][:])
+            nc.sync.dma_start(out=out_rows[:, j, c0:c1], in_=res[:])
 
         far_first = [4, 5, 0, 1, 2, 3]
         v_copy, s_copy = nc.vector.tensor_copy, nc.scalar.copy
@@ -268,21 +275,20 @@ def tile_hic_compartment_scores_s2_kernel(
         load_oe(1)
         load_w(0)
         load_w(1)
-        load_w(2)
-        load_trans(0)
-        load_w(3)
         load_oe(2)
-        load_w(4)
-        load_w(5)
+        load_trans(0)
+        load_w(2)
+        load_oe(3)
+        load_w(3)
         load_trans(1)
+        load_w(4)
+        load_oe(4)
         nc.sync.dma_start(out=root_col[:], in_=inv_root.rearrange("(p a) -> p a", p=P))
         nc.sync.dma_start(out=sd_col[:], in_=inv_sd.rearrange("(p j) -> p j", p=P))
-        load_oe(3)
         load_trans(2)
-        load_oe(4)
-        load_trans(3)
+        load_w(5)
         load_oe(5)
-        load_trans(4)
+        load_trans(3)
 
         weight_table(0)
         weight_table(1)
@@ -291,7 +297,8 @@ def tile_hic_compartment_scores_s2_kernel(
         nc.vector.tensor_scalar(out=minus_mean[:], in0=mean_col[:], scalar1=-1.0, scalar2=None, op0=MULT)
         centre(0, 0, 256)
         centre(0, 256, 512)
-        centre(0, 512, 1024)
+        centre(0, 512, 768)
+        centre(0, 768, 1024)
         log_of(1, 0, 2)
         log_of(1, 1, 2)
         if GP:
@@ -300,7 +307,7 @@ def tile_hic_compartment_scores_s2_kernel(
         interleave_w(0, g_copy, 0, GC)
         centre(1, 0, 512)
         centre(1, 512, 1024)
-        cis_first = [0, 1, 2, 3, 4, 5]
+        in_order = [0, 1, 2, 3, 4, 5]
         turn_z(0, 0)
         turn_z(0, 1)
         empty_z(0, 0)
@@ -308,51 +315,83 @@ def tile_hic_compartment_scores_s2_kernel(
         turn_z(1, 0)
         turn_z(1, 1)
         turn_trans(0)
-        interleave_w(1, s_copy)
-        interleave_w(2, v_copy)
-        if GC < N:
-            interleave_w(0, v_copy, GC, N)
-        quantize_w(0)
-        quantize_z(0)
-        multiply(0, cis_first, 0, 1)
+        if SW:
+            interleave_w(1, s_copy)
+        log_of(2)
+        load_oe(6)
+        load_trans(4)
         empty_z(1, 0)
         empty_z(1, 1)
-        interleave_w(3, v_copy)
-        quantize_w(1)
-        quantize_w(2)
-        multiply(0, cis_first, 1, 3)
-        quantize_z(1)
-        multiply(1, cis_first, 0, 3)
-        log_of(2)
         empty_trans(0)
-        quantize_w(3)
-        multiply(0, cis_first, 3, 4)
-        multiply(1, cis_first, 3, 4)
-        interleave_w(4, g_copy, 0, GC4)
-        turn_trans(1)
-        interleave_w(5, s_copy)
+        log_of(3)
+        load_oe(7)
+        interleave_w(0, v_copy, GC, N)
+        if not SW:
+            interleave_w(1, v_copy)
+        quantize_w(0)
+        quantize_z(0)
+        quantize_w(1)
+        interleave_w(2, g_copy, 0, GC)
         centre(2, 0, 1024)
-        root_table()
-        empty_trans(1, v_copy)
-        if GC4 < N:
-            interleave_w(4, v_copy, GC4, N)
-        quantize_trans(0)
-        quantize_w(4)
-        quantize_w(5)
+        turn_trans(1)
+        multiply(0, in_order, 0, 2)
+        empty_trans(1)
+        if SR >= 1:
+            interleave_w(2, s_copy, GC, N)
         turn_z(2, 0)
         turn_z(2, 1)
-        turn_trans(2)
-        multiply(0, cis_first, 4, 6)
-        log_of(3)
+        log_of(4)
         empty_z(2, 0)
         empty_z(2, 1)
+        if SR < 1:
+            interleave_w(2, v_copy, GC, N)
+        interleave_w(3, v_copy)
+        quantize_trans(0)
+        quantize_z(1)
+        quantize_w(2)
+        quantize_w(3)
+        interleave_w(4, g_copy, 0, GC)
+        centre(3, 0, 1024)
+        turn_trans(2)
+        multiply(1, in_order, 0, 2)
+        multiply(0, in_order, 2, 4)
+        multiply(1, in_order, 2, 4)
         empty_trans(2)
-
+        root_table()
         turn_trans(3)
+        if SR >= 2:
+            interleave_w(4, s_copy, GC, N)
+        log_of(5)
+        empty_trans(3)
+        turn_z(3, 0)
+        turn_z(3, 1)
+        if SR < 2:
+            interleave_w(4, v_copy, GC, N)
+        quantize_trans(1)
+        quantize_trans(2)
+        quantize_w(4)
+        interleave_w(5, g_copy, 0, GC)
+        centre(4, 0, 1024)
+        multiply(0, in_order, 4, 5)
+        multiply(1, in_order, 4, 5)
+        turn_trans(4)
+        empty_z(3, 0)
+        empty_z(3, 1)
+        load_trans(5)
+        load_trans(6)
+        load_trans(7)
+        load_trans(8)
+        if SR >= 3:
+            interleave_w(5, s_copy, GC, N)
+        if LD == 2:
+            log_of(6)
+        empty_trans(4)
+        if SR < 3:
+            interleave_w(5, v_copy, GC, N)
         last = TILES - 1
 
         def on_vector(s):
-            return V_EMPTY and s > 2 and (s % V_EMPTY == 0) == VG
+            return V_EMPTY and s > 4 and (s % V_EMPTY == 0) == VG
 
         def centre_step(s):
             if GP and G_FROM <= s <= G_TO:
@@ -362,64 +401,88 @@ def tile_hic_compartment_scores_s2_kernel(
                 centre(s, 0, 1024)
 
         def load_step(s):
-            if s + 2 < TILES:
-                load_trans(s + 2)
+            if s + 4 < TILES:
+                load_trans(s + 4)
             if s + 3 < TILES:
                 load_oe(s + 3)
 
-        for s in range(3, last):
+        for s in range(5, last - 1):
             load_step(s)
-            if s > 4:
-                quantize_z(s - 3)
+            quantize_z(s - 3)
+            if s == 5:
+                quantize_w(5)
             quantize_trans(s - 2)
-            if s == 3:
-                multiply(1, cis_first, 4, 6)
-            elif s > 4:
+            if s == 5:
+                multiply(0, in_order, 5)
+                multiply(1, in_order, 5)
+            else:
                 multiply(s - 3, far_first, 2)
             centre_step(s)
-            log_of(s + 1, 0, 1 if s + 1 < last else 2)
+            if s + LD < TILES and s < LS:
+                log_of(s + LD)
             if on_vector(s - 1):
                 empty_trans(s - 1, v_copy)
-            finish(s - 3)
-            if s > 3:
-                turn_z(s - 1, 0)
-                turn_z(s - 1, 1)
-                turn_trans(s)
-                if s + 1 < last:
-                    multiply(s - 2, far_first, 0, 2)
-                if s + 1 == last:
-                    log_of(last, 1, 2)
-                empty_z(s - 1, 0)
-                empty_z(s - 1, 1)
+            if s == 5:
+                finish(0)
+            if FL == 4 or s < 7:
+                finish(s - 4)
+            if FL == 3 and s >= 6:
+                finish(s - 3)
+            turn_z(s - 1, 0)
+            turn_z(s - 1, 1)
+            turn_trans(s)
+            if s == 5:
+                multiply(2, far_first)
+            if s >= ET and s < ET + 2:
+                turn_trans(last - 1 + s - ET)
+            multiply(s - 2, far_first, 0, 2)
+            empty_z(s - 1, 0)
+            empty_z(s - 1, 1)
             if not on_vector(s):
                 empty_trans(s)
-        quantize_z(last - 3)
-        multiply(last - 3, far_first)
-        if on_vector(last - 1):
-            empty_trans(last - 1)
+            if s >= LS:
+                log_of(s + LD)
+            if s >= ET and s < ET + 2:
+                empty_trans(last - 1 + s - ET)
+            if s == last - 2:
+                finish(s - 3)
+        s = last - 1
+        if on_vector(s - 1):
+            empty_trans(s - 1)
+        quantize_z(s - 3)
+        multiply(s - 3, far_first, 2)
+        quantize_z(s - 2)
+        quantize_trans(s - 1)
+        quantize_trans(s - 2)
+        centre_step(s)
+        turn_z(s - 1, 0)
+        turn_z(s - 1, 1)
+        multiply(s - 2, far_first)
+        empty_z(s - 1, 0)
+        empty_z(s - 1, 1)
+        finish(s - 3)
         turn_z(last - 1, 0)
         turn_z(last - 1, 1)
-        centre(last, 0, 512)
-        quantize_z(last - 2)
-        quantize_trans(last - 2)
-        centre(last, 512, 1024)
         empty_z(last - 1, 0)
         empty_z(last - 1, 1)
-        turn_trans(last)
+        quantize_z(last - 2)
+        quantize_trans(last - 1)
+        multiply(last - 2, far_first)
+        centre(last, 0, 512)
         turn_z(last, 0)
-        finish(last - 3)
-        multiply(last - 2, far_first, 0, TM)
-        empty_trans(last)
         empty_z(last, 0)
+        quantize_z(last - 1)
+        quantize_trans(last)
+        multiply(last - 1, far_first, 0, TM)
+        centre(last, 512, 1024)
         turn_z(last, 1)
         empty_z(last, 1)
-        multiply(last - 2, far_first, TM)
-        quantize_trans(last - 1)
-        quantize_z(last - 1)
-        multiply(last - 1, far_first)
-        quantize_trans(last)
-        quantize_z(last)
+        multiply(last - 1, far_first, TM)
+        quantize_z(last, 0, 2)
+        finish(last - 3)
         finish(last - 2)
+        quantize_z(last, 1, 2)
         multiply(last, far_first)
         finish(last - 1)
-        finish(last)
+        finish(last, 0, N // 2)
+        finish(last, N // 2, N)

@@ -29,6 +29,10 @@ TAPER = 11
 GC = 384
 GC4 = 384
 TM = 4
+QT = 0
+LH = 2
+VL = 13
+VO = 0
 AT = 2
 ET = 10
 LS = 13
@@ -37,14 +41,14 @@ LD = 2
 FL = 4
 SR = 2
 LEAD = 1
-GP = 208
+GP = 240
 G_FROM = 5
 G_TO = 14
-V_EMPTY = 2
+V_EMPTY = 3
 SPLIT = 0
 TURN = 4
 GW = 1
-VG = 1
+VG = 0
 
 
 def tile_hic_compartment_scores_s2_kernel(
@@ -182,10 +186,10 @@ def tile_hic_compartment_scores_s2_kernel(
                 op=MULT,
             )
 
-        def turn_z(j, h):
+        def turn_z(j, h, g0=0, g1=2):
             words = z_t[j][:].bitcast(F32)
             zbank[j, h] = psum.tile([P, 4, P], F32, name="turn", bufs=TURN)
-            for g in range(2):
+            for g in range(g0, g1):
                 for u in range(2):
                     c0 = u * 512 + (2 * h + g) * P
                     nc.tensor.transpose(zbank[j, h][:, 2 * g + u, :], words[:, c0 : c0 + P], ident[:])
@@ -209,6 +213,12 @@ def tile_hic_compartment_scores_s2_kernel(
             if h == 0:
                 zg[j] = work.tile([P, K], BF16, name="zg", bufs=4, align_bytes=64)
             empty(zbank[j, h], zg[j][:, h * 1024 : (h + 1) * 1024], copy)
+
+        def empty_pass(j, g):
+            nc.scalar.copy(
+                out=zg[j][:, g * 512 : (g + 1) * 512].bitcast(F32).rearrange("p (r u) -> p r u", u=2),
+                in_=zbank[j, g // 2][:, 2 * (g % 2) : 2 * (g % 2) + 2, :].rearrange("p u r -> p r u"),
+            )
 
         def empty_trans(j, copy=nc.scalar.copy):
             tg[j] = work.tile([P, T], BF16, name="tg", tag="tg%d" % (j % 2 if j < TILES - 2 else j), bufs=1, align_bytes=64)
@@ -391,7 +401,7 @@ def tile_hic_compartment_scores_s2_kernel(
         last = TILES - 1
 
         def on_vector(s):
-            return V_EMPTY and s > 4 and (s % V_EMPTY == 0) == VG
+            return V_EMPTY and 4 < s < VL and ((s + VO) % V_EMPTY == 0) == VG
 
         def centre_step(s):
             if GP and G_FROM <= s <= G_TO:
@@ -441,7 +451,7 @@ def tile_hic_compartment_scores_s2_kernel(
             if not on_vector(s):
                 empty_trans(s)
             if s >= LS:
-                log_of(s + LD)
+                log_of(s + LD, 0, LH)
             if s >= ET and s < ET + 2:
                 empty_trans(last - 1 + s - ET)
             if s == last - 2:
@@ -460,6 +470,8 @@ def tile_hic_compartment_scores_s2_kernel(
         multiply(s - 2, far_first)
         empty_z(s - 1, 0)
         empty_z(s - 1, 1)
+        if LH == 2:
+            log_of(last, 1, 2)
         finish(s - 3)
         turn_z(last - 1, 0)
         turn_z(last - 1, 1)
@@ -474,14 +486,28 @@ def tile_hic_compartment_scores_s2_kernel(
         quantize_z(last - 1)
         quantize_trans(last)
         multiply(last - 1, far_first, 0, TM)
-        centre(last, 512, 1024)
-        turn_z(last, 1)
-        empty_z(last, 1)
-        multiply(last - 1, far_first, TM)
-        quantize_z(last, 0, 2)
-        finish(last - 3)
-        finish(last - 2)
-        quantize_z(last, 1, 2)
+        if QT:
+            centre(last, 512, 768)
+            turn_z(last, 1, 0, 1)
+            empty_pass(last, 2)
+            centre(last, 768, 1024)
+            turn_z(last, 1, 1, 2)
+            empty_pass(last, 3)
+            multiply(last - 1, far_first, TM)
+            quantize_z(last, 0, 2)
+            finish(last - 3)
+            quantize_z(last, 2, 4)
+            quantize_z(last, 3, 4)
+            finish(last - 2)
+        else:
+            centre(last, 512, 1024)
+            turn_z(last, 1)
+            empty_z(last, 1)
+            multiply(last - 1, far_first, TM)
+            quantize_z(last, 0, 2)
+            finish(last - 3)
+            finish(last - 2)
+            quantize_z(last, 1, 2)
         multiply(last, far_first)
         finish(last - 1)
         finish(last, 0, N // 2)

from contextlib import ExitStack

import concourse.mybir as mybir
from concourse.masks import make_identity

M, K, T, N = 2048, 2048, 1024, 512
FLOPS = 2 * M * (K + T) * N

F32 = mybir.dt.float32
BF16 = mybir.dt.bfloat16
U32 = mybir.dt.uint32
U8 = mybir.dt.uint8
E4M3 = mybir.dt.float8_e4m3fn_x4
E5M2 = mybir.dt.float8_e5m2_x4
LN = mybir.ActivationFunctionType.Ln
SUB = mybir.AluOpType.subtract
ADD = mybir.AluOpType.add
MULT = mybir.AluOpType.mult

P = 128
PACK = 4
K_PASS = P * PACK
TILES = M // P
CIS_PASSES = K // K_PASS
FAR_PASSES = T // K_PASS
PASSES = CIS_PASSES + FAR_PASSES
CATCH = 10
TAPER = 11
GC = 384
GC4 = 384
TM = 4
QT = 0
LH = 2
VL = 13
VO = 0
AT = 2
ET = 10
LS = 13
SW = 0
LD = 2
FL = 4
SR = 2
LEAD = 1
GP = 240
G_FROM = 5
G_TO = 14
V_EMPTY = 3
SPLIT = 0
TURN = 4
GW = 1
VG = 0


def tile_hic_compartment_scores_s2_kernel(
    tc, oe, row_mean, bin_weight, trans, cis_load, trans_load, inv_sd, inv_root, out
):
    nc = tc.nc
    oe_rows = oe.rearrange("(p j) k -> p j k", j=TILES)
    trans_rows = trans.rearrange("(p j) k -> p j k", j=TILES)
    out_rows = out.rearrange("(p j) c -> p j c", j=TILES)

    with ExitStack() as ctx:
        keep = ctx.enter_context(tc.tile_pool(name="keep", bufs=1))
        work = ctx.enter_context(tc.tile_pool(name="work", bufs=2))
        psum = ctx.enter_context(tc.psum_pool(name="psum", bufs=2))
        ctx.enter_context(tc.manual_schedule())

        ident = keep.tile([P, P], F32, name="ident")
        mean_col = keep.tile([P, TILES], BF16, name="mean_col")
        minus_mean = keep.tile([P, TILES], F32, name="minus_mean")
        sd_col = keep.tile([P, TILES], BF16, name="sd_col")
        weight_col = keep.tile([P, K // P], BF16, name="weight_col")
        root_col = keep.tile([P, N // P], BF16, name="root_col")
        weight_row = keep.tile([P, 2, max(GP, 16)], BF16, name="weight_row", align_bytes=64)
        weight_bank = {}
        gate_slot = {}
        root_row = keep.tile([P, N], BF16, name="root_row", align_bytes=64)

        oe_t, tr_t, ln_t, z_t, zbank, tbank, zg, tg, zq, tq, acc = ({} for i in range(11))
        w_raw, w_int, w_q = {}, {}, {}

        def load_oe(j, parts=1):
            tiles = []
            width = K // parts
            for h in range(parts):
                if parts == 1:
                    t = work.tile([P, width], BF16, name="oe", bufs=6)
                else:
                    t = work.tile([P, width], BF16, name="oe_part", bufs=4)
                nc.sync.dma_start(out=t[:], in_=oe_rows[:, j, h * width : (h + 1) * width])
                tiles.append(t)
            oe_t[j] = tiles

        def load_trans(j):
            tr_t[j] = work.tile([P, T], BF16, name="tr", bufs=7)
            nc.sync.dma_start(out=tr_t[j][:], in_=trans_rows[:, j, :])

        def load_w(g):
            src = cis_load if g < CIS_PASSES else trans_load
            g0 = g if g < CIS_PASSES else g - CIS_PASSES
            w_raw[g] = work.tile([P, PACK * N], BF16, name="w_raw", bufs=PASSES)
            nc.sync.dma_start(
                out=w_raw[g][:],
                in_=src[g0 * K_PASS : (g0 + 1) * K_PASS, :].rearrange("(p t) c -> p (t c)", t=PACK),
            )

        def g_copy(out, in_):
            nc.gpsimd.tensor_scalar(out=out, in0=in_, scalar1=1.0, scalar2=0.0, op0=MULT, op1=ADD)

        def interleave_w(g, copy, c0=0, c1=N):
            if c0 == 0:
                w_int[g] = work.tile([P, N * PACK], BF16, name="w_int", tag="wi%d" % (g in (1, 2)), bufs=1, align_bytes=64)
            copy(
                out=w_int[g][:].rearrange("p (c i t) -> p c t i", i=4, t=PACK)[:, c0 // 4 : c1 // 4],
                in_=w_raw[g][:].rearrange("p (t c i) -> p c t i", i=4, t=PACK)[:, c0 // 4 : c1 // 4],
            )

        def quantize_w(g):
            codes = keep.tile([P, N], U32, name="w_codes", bufs=PASSES, align_bytes=64)
            scales = keep.tile([P, N], U8, name="w_scales", bufs=PASSES, align_bytes=64)
            nc.vector.quantize_mx(out=codes[:].bitcast(E4M3), scales=scales[:], in_=w_int[g][:])
            w_q[g] = (codes, scales)

        def spread(col, a, dst):
            words = col[:].bitcast(F32)
            nc.tensor.transpose(dst, words[:, a : a + 1].to_broadcast([P, P]), ident[:])

        def weight_table(u):
            weight_bank[u] = psum.tile([P, 512], F32, name="wbank", bufs=2)
            for a in range(4):
                spread(weight_col, 2 * a + u, weight_bank[u][:, a:512:4])

        def weight_share(u):
            nc.vector.tensor_copy(
                out=weight_row[:, u, :].bitcast(F32), in_=weight_bank[u][:, 512 - GP // 2 : 512]
            )

        def root_table():
            bank = psum.tile([P, 4, P], F32, name="turn", bufs=TURN)
            for a in range(2):
                spread(root_col, a, bank[:, a, :])
            nc.vector.tensor_copy(
                out=root_row[:].bitcast(F32).rearrange("p (n a) -> p n a", a=2),
                in_=bank[:, 0:2, :].rearrange("p a n -> p n a"),
            )

        def log_of(j, h=0, parts=1):
            if h == 0:
                ln_t[j] = work.tile([P, K], F32, name="ln", bufs=4)
            pairs = K // PACK // parts
            src = oe_t[j][h] if len(oe_t[j]) > 1 else oe_t[j][0][:, h * (K // parts) : (h + 1) * (K // parts)]
            nc.scalar.activation(
                out=ln_t[j][:].rearrange("p (u m e) -> p u m e", u=2, e=2)[:, :, h * pairs : (h + 1) * pairs, :],
                in_=src[:].rearrange("p (m u e) -> p u m e", u=2, e=2),
                func=LN,
            )

        def centre(j, c0, c1):
            if c0 == 0:
                z_t[j] = work.tile([P, K], BF16, name="z", bufs=3)
            for u in range(2):
                cols = slice(u * 1024 + c0, u * 1024 + c1)
                nc.vector.scalar_tensor_tensor(
                    out=z_t[j][:, cols],
                    in0=ln_t[j][:, cols],
                    scalar=mean_col[:, j : j + 1],
                    in1=weight_bank[u][:].bitcast(BF16)[:, c0:c1],
                    op0=SUB,
                    op1=MULT,
                )

        def centre_share(j):
            diff = work.tile([P, 2, GP], F32, name="diff", tag="tg%d" % (j % 2), bufs=1, align_bytes=64)
            nc.gpsimd.tensor_scalar(
                out=diff[:],
                in0=ln_t[j][:].rearrange("p (u x) -> p u x", u=2)[:, :, 1024 - GP : 1024],
                scalar1=minus_mean[:, j : j + 1],
                scalar2=1.0,
                op0=ADD,
                op1=MULT,
            )
            nc.gpsimd.tensor_tensor(
                out=z_t[j][:].rearrange("p (u x) -> p u x", u=2)[:, :, 1024 - GP : 1024],
                in0=diff[:],
                in1=weight_row[:],
                op=MULT,
            )

        def turn_z(j, h, g0=0, g1=2):
            words = z_t[j][:].bitcast(F32)
            zbank[j, h] = psum.tile([P, 4, P], F32, name="turn", bufs=TURN)
            for g in range(g0, g1):
                for u in range(2):
                    c0 = u * 512 + (2 * h + g) * P
                    nc.tensor.transpose(zbank[j, h][:, 2 * g + u, :], words[:, c0 : c0 + P], ident[:])

        def turn_trans(j):
            words = tr_t[j][:].bitcast(F32)
            tbank[j] = psum.tile([P, 4, P], F32, name="turn", bufs=TURN)
            for g in range(2):
                for u in range(2):
                    nc.tensor.transpose(
                        tbank[j][:, 2 * g + u, :], words[:, 256 * g + u : 256 * (g + 1) : 2], ident[:]
                    )

        def empty(bank, dst, copy):
            copy(
                out=dst.bitcast(F32).rearrange("p (g r u) -> p g r u", g=2, u=2),
                in_=bank[:].rearrange("p (g u) r -> p g r u", u=2),
            )

        def empty_z(j, h, copy=nc.scalar.copy):
            if h == 0:
                zg[j] = work.tile([P, K], BF16, name="zg", bufs=4, align_bytes=64)
            empty(zbank[j, h], zg[j][:, h * 1024 : (h + 1) * 1024], copy)

        def empty_pass(j, g):
            nc.scalar.copy(
                out=zg[j][:, g * 512 : (g + 1) * 512].bitcast(F32).rearrange("p (r u) -> p r u", u=2),
                in_=zbank[j, g // 2][:, 2 * (g % 2) : 2 * (g % 2) + 2, :].rearrange("p u r -> p r u"),
            )

        def empty_trans(j, copy=nc.scalar.copy):
            tg[j] = work.tile([P, T], BF16, name="tg", tag="tg%d" % (j % 2 if j < TILES - 2 else j), bufs=1, align_bytes=64)
            empty(tbank[j], tg[j][:], copy)

        def quantize_z(j, h=0, parts=1):
            if h == 0:
                codes = work.tile([P, K // PACK], U32, name="z_codes", bufs=4, align_bytes=64)
                scales = work.tile([P, K // PACK], U8, name="z_scales", bufs=4, align_bytes=64)
                zq[j] = (codes, scales)
            codes, scales = zq[j]
            w = K // PACK // parts
            nc.vector.quantize_mx(
                out=codes[:, h * w : (h + 1) * w].bitcast(E4M3),
                scales=scales[:, h * w : (h + 1) * w],
                in_=zg[j][:, h * w * PACK : (h + 1) * w * PACK],
            )

        def quantize_trans(j):
            codes = work.tile([P, T // PACK], U32, name="t_codes", bufs=4, align_bytes=64)
            scales = work.tile([P, T // PACK], U8, name="t_scales", bufs=4, align_bytes=64)
            nc.vector.quantize_mx(out=codes[:].bitcast(E5M2), scales=scales[:], in_=tg[j][:])
            tq[j] = (codes, scales)

        def multiply(j, order, lo=0, hi=PASSES):
            if lo == 0 and j >= TILES - AT:
                acc[j] = psum.tile([P, N], F32, name="turn", bufs=TURN)
            elif lo == 0:
                acc[j] = psum.tile([P, N], F32, name="acc", bufs=6 - TURN)
            for g in order[lo:hi]:
                if g < CIS_PASSES:
                    (codes, scales), fmt, c0 = zq[j], E4M3, g * P
                else:
                    (codes, scales), fmt, c0 = tq[j], E5M2, (g - CIS_PASSES) * P
                nc.tensor.matmul_mx(
                    out=acc[j][:],
                    lhsT=codes[:, c0 : c0 + P].bitcast(fmt),
                    lhsT_scale=scales[:, c0 : c0 + P],
                    rhs=w_q[g][0][:].bitcast(E4M3),
                    rhs_scale=w_q[g][1][:],
                    start=(g == order[0]),
                    stop=(g == order[-1]),
                )

        def finish(j, c0=0, c1=N):
            res = work.tile([P, c1 - c0], F32, name="res", bufs=6)
            nc.vector.scalar_tensor_tensor(
                out=res[:],
                in0=acc[j][:, c0:c1],
                scalar=sd_col[:, j : j + 1],
                in1=root_row[:, c0:c1],
                op0=MULT,
                op1=MULT,
            )
            nc.sync.dma_start(out=out_rows[:, j, c0:c1], in_=res[:])

        far_first = [4, 5, 0, 1, 2, 3]
        v_copy, s_copy = nc.vector.tensor_copy, nc.scalar.copy

        make_identity(nc, ident[:])
        nc.sync.dma_start(out=weight_col[:], in_=bin_weight.rearrange("(p a) -> p a", p=P))
        nc.sync.dma_start(out=mean_col[:], in_=row_mean.rearrange("(p j) -> p j", p=P))
        load_oe(0, parts=4)
        load_oe(1)
        load_w(0)
        load_w(1)
        load_oe(2)
        load_trans(0)
        load_w(2)
        load_oe(3)
        load_w(3)
        load_trans(1)
        load_w(4)
        load_oe(4)
        nc.sync.dma_start(out=root_col[:], in_=inv_root.rearrange("(p a) -> p a", p=P))
        nc.sync.dma_start(out=sd_col[:], in_=inv_sd.rearrange("(p j) -> p j", p=P))
        load_trans(2)
        load_w(5)
        load_oe(5)
        load_trans(3)

        weight_table(0)
        weight_table(1)
        for h in range(4):
            log_of(0, h, 4)
        nc.vector.tensor_scalar(out=minus_mean[:], in0=mean_col[:], scalar1=-1.0, scalar2=None, op0=MULT)
        centre(0, 0, 256)
        centre(0, 256, 512)
        centre(0, 512, 768)
        centre(0, 768, 1024)
        log_of(1, 0, 2)
        log_of(1, 1, 2)
        if GP:
            weight_share(0)
            weight_share(1)
        interleave_w(0, g_copy, 0, GC)
        centre(1, 0, 512)
        centre(1, 512, 1024)
        in_order = [0, 1, 2, 3, 4, 5]
        turn_z(0, 0)
        turn_z(0, 1)
        empty_z(0, 0)
        empty_z(0, 1)
        turn_z(1, 0)
        turn_z(1, 1)
        turn_trans(0)
        if SW:
            interleave_w(1, s_copy)
        log_of(2)
        load_oe(6)
        load_trans(4)
        empty_z(1, 0)
        empty_z(1, 1)
        empty_trans(0)
        log_of(3)
        load_oe(7)
        interleave_w(0, v_copy, GC, N)
        if not SW:
            interleave_w(1, v_copy)
        quantize_w(0)
        quantize_z(0)
        quantize_w(1)
        interleave_w(2, g_copy, 0, GC)
        centre(2, 0, 1024)
        turn_trans(1)
        multiply(0, in_order, 0, 2)
        empty_trans(1)
        if SR >= 1:
            interleave_w(2, s_copy, GC, N)
        turn_z(2, 0)
        turn_z(2, 1)
        log_of(4)
        empty_z(2, 0)
        empty_z(2, 1)
        if SR < 1:
            interleave_w(2, v_copy, GC, N)
        interleave_w(3, v_copy)
        quantize_trans(0)
        quantize_z(1)
        quantize_w(2)
        quantize_w(3)
        interleave_w(4, g_copy, 0, GC)
        centre(3, 0, 1024)
        turn_trans(2)
        multiply(1, in_order, 0, 2)
        multiply(0, in_order, 2, 4)
        multiply(1, in_order, 2, 4)
        empty_trans(2)
        root_table()
        turn_trans(3)
        if SR >= 2:
            interleave_w(4, s_copy, GC, N)
        log_of(5)
        empty_trans(3)
        turn_z(3, 0)
        turn_z(3, 1)
        if SR < 2:
            interleave_w(4, v_copy, GC, N)
        quantize_trans(1)
        quantize_trans(2)
        quantize_w(4)
        interleave_w(5, g_copy, 0, GC)
        centre(4, 0, 1024)
        multiply(0, in_order, 4, 5)
        multiply(1, in_order, 4, 5)
        turn_trans(4)
        empty_z(3, 0)
        empty_z(3, 1)
        load_trans(5)
        load_trans(6)
        load_trans(7)
        load_trans(8)
        if SR >= 3:
            interleave_w(5, s_copy, GC, N)
        if LD == 2:
            log_of(6)
        empty_trans(4)
        if SR < 3:
            interleave_w(5, v_copy, GC, N)
        last = TILES - 1

        def on_vector(s):
            return V_EMPTY and 4 < s < VL and ((s + VO) % V_EMPTY == 0) == VG

        def centre_step(s):
            if GP and G_FROM <= s <= G_TO:
                centre(s, 0, 1024 - GP)
                centre_share(s)
            else:
                centre(s, 0, 1024)

        def load_step(s):
            if s + 4 < TILES:
                load_trans(s + 4)
            if s + 3 < TILES:
                load_oe(s + 3)

        for s in range(5, last - 1):
            load_step(s)
            quantize_z(s - 3)
            if s == 5:
                quantize_w(5)
            quantize_trans(s - 2)
            if s == 5:
                multiply(0, in_order, 5)
                multiply(1, in_order, 5)
            else:
                multiply(s - 3, far_first, 2)
            centre_step(s)
            if s + LD < TILES and s < LS:
                log_of(s + LD)
            if on_vector(s - 1):
                empty_trans(s - 1, v_copy)
            if s == 5:
                finish(0)
            if FL == 4 or s < 7:
                finish(s - 4)
            if FL == 3 and s >= 6:
                finish(s - 3)
            turn_z(s - 1, 0)
            turn_z(s - 1, 1)
            turn_trans(s)
            if s == 5:
                multiply(2, far_first)
            if s >= ET and s < ET + 2:
                turn_trans(last - 1 + s - ET)
            multiply(s - 2, far_first, 0, 2)
            empty_z(s - 1, 0)
            empty_z(s - 1, 1)
            if not on_vector(s):
                empty_trans(s)
            if s >= LS:
                log_of(s + LD, 0, LH)
            if s >= ET and s < ET + 2:
                empty_trans(last - 1 + s - ET)
            if s == last - 2:
                finish(s - 3)
        s = last - 1
        if on_vector(s - 1):
            empty_trans(s - 1)
        quantize_z(s - 3)
        multiply(s - 3, far_first, 2)
        quantize_z(s - 2)
        quantize_trans(s - 1)
        quantize_trans(s - 2)
        centre_step(s)
        turn_z(s - 1, 0)
        turn_z(s - 1, 1)
        multiply(s - 2, far_first)
        empty_z(s - 1, 0)
        empty_z(s - 1, 1)
        if LH == 2:
            log_of(last, 1, 2)
        finish(s - 3)
        turn_z(last - 1, 0)
        turn_z(last - 1, 1)
        empty_z(last - 1, 0)
        empty_z(last - 1, 1)
        quantize_z(last - 2)
        quantize_trans(last - 1)
        multiply(last - 2, far_first)
        centre(last, 0, 512)
        turn_z(last, 0)
        empty_z(last, 0)
        quantize_z(last - 1)
        quantize_trans(last)
        multiply(last - 1, far_first, 0, TM)
        if QT:
            centre(last, 512, 768)
            turn_z(last, 1, 0, 1)
            empty_pass(last, 2)
            centre(last, 768, 1024)
            turn_z(last, 1, 1, 2)
            empty_pass(last, 3)
            multiply(last - 1, far_first, TM)
            quantize_z(last, 0, 2)
            finish(last - 3)
            quantize_z(last, 2, 4)
            quantize_z(last, 3, 4)
            finish(last - 2)
        else:
            centre(last, 512, 1024)
            turn_z(last, 1)
            empty_z(last, 1)
            multiply(last - 1, far_first, TM)
            quantize_z(last, 0, 2)
            finish(last - 3)
            finish(last - 2)
            quantize_z(last, 1, 2)
        multiply(last, far_first)
        finish(last - 1)
        finish(last, 0, N // 2)
        finish(last, N // 2, N)
